import numpy as np
import ml_dtypes


def mxq(x, axis, fmt="e4m3"):
    dtype, down = {"e4m3": (ml_dtypes.float8_e4m3fn, 7), "e5m2": (ml_dtypes.float8_e5m2, 14)}[fmt]
    v = np.moveaxis(np.asarray(x, np.float32).astype(ml_dtypes.bfloat16).astype(np.float64), axis, -1)
    blocks = v.reshape(v.shape[:-1] + (-1, 32))
    amax = np.abs(blocks).max(-1, keepdims=True)
    byte = np.maximum(np.where(amax > 0, np.frexp(amax)[1] - 1 + 127, 0) - down, 1)
    scale = np.exp2(byte - 127.0)
    codes = (blocks / scale).astype(np.float32).astype(dtype).astype(np.float64)
    return np.moveaxis((codes * scale).reshape(v.shape), -1, axis)


WIDE = False


def mx_kscale(k):
    if not WIDE:
        return np.ones(k)
    levels = np.array([30, -30])
    if k % 512:
        return np.exp2(np.random.permutation(np.resize(levels, k // 32))).repeat(32)
    a = np.empty((k // 512, 16))
    for p in range(k // 512):
        a[p, :8] = np.random.permutation(np.resize(levels, 8))
        for g in range(8):
            far = levels[np.abs(levels - a[p, g]) >= 10]
            a[p, g + 8] = far[np.random.randint(len(far))]
    return np.exp2(a.ravel()).repeat(32)


def f64(x):
    return np.asarray(x).astype(np.float64)


def striped(idx):
    return np.tile(np.asarray(idx).reshape(-1, 16).T, (8, 1)).astype(np.uint16)


def unstriped(offs):
    return offs[:16].T.reshape(-1).astype(np.int64)


E2M1 = np.array([0.0, 0.5, 1.0, 1.5, 2.0, 3.0, 4.0, 6.0, -0.0, -0.5, -1.0, -1.5, -2.0, -3.0, -4.0, -6.0])


def pack_weight(w, fmt):
    k, n = w.shape
    w = f64(np.asarray(w, np.float32).astype(ml_dtypes.bfloat16)).reshape(k // 32, 32, n)
    amax = np.abs(w).max(1)
    if fmt in ("e4m3", "e5m2"):
        byte = np.frexp(amax)[1] - 1 + 127 - (7 if fmt == "e4m3" else 14)
    else:
        mant, ex = np.frexp(amax / 6.0)
        byte = np.where(mant > 0.5, ex, ex - 1) + 127
    byte = np.clip(np.where(amax > 0, byte, 1), 1, 254)
    scaled = (w * np.exp2(127.0 - byte)[:, None, :]).reshape(k, n).astype(np.float32)
    by_word = np.ascontiguousarray(scaled.reshape(k // 512, 128, 4, n).transpose(0, 1, 3, 2))
    if fmt in ("e4m3", "e5m2"):
        words = by_word.astype(ml_dtypes.float8_e4m3fn if fmt == "e4m3" else ml_dtypes.float8_e5m2).view(np.uint8)
    else:
        c = by_word.astype(ml_dtypes.float4_e2m1fn).view(np.uint8) & 0xF
        words = (c[..., 0::2] | (c[..., 1::2] << 4)).reshape(k // 512, 128, 2 * n)
    return np.ascontiguousarray(words), np.ascontiguousarray(byte.astype(np.uint8).reshape(k // 512, 16, n))


def unpack_weight(words, scales, fmt):
    g, _, n = scales.shape
    words = np.ascontiguousarray(words).reshape(g, 128, n, -1)
    if fmt in ("e4m3", "e5m2"):
        vals = words.view(ml_dtypes.float8_e4m3fn if fmt == "e4m3" else ml_dtypes.float8_e5m2).astype(np.float64)
    else:
        nib = np.empty((g, 128, n, 4), np.uint8)
        nib[..., 0::2] = words & 0xF
        nib[..., 1::2] = words >> 4
        vals = E2M1[nib]
    vals = vals * np.repeat(np.exp2(scales.astype(np.float64) - 127.0), 8, axis=1)[..., None]
    return vals.transpose(0, 1, 3, 2).reshape(g * 512, n)


K, T, J, R, O, N, E = 512, 2048, 256, 512, 128, 256, 1024


def setup_inputs():
    n = np.random.standard_normal
    idx = np.random.permutation(T)[:J]
    idx2 = np.random.permutation(T)[:J]
    idx3 = np.random.permutation(T)[:J]
    idx4 = np.random.permutation(J)[:O]
    idx5 = np.random.permutation(J)[:O]
    idx6 = np.random.permutation(E)[:O]
    fk = mx_kscale(K)
    fr = mx_kscale(R)
    xtp = pack_weight(n((K, T)) / fk[:, None], "e4m3")
    wp = pack_weight(n((K, R)) * 1 / np.sqrt(K) * fk[:, None] * fr, "e2m1")
    wbp = pack_weight(n((R, N)) * 1 / np.sqrt(R) / fr[:, None], "e5m2")
    return {
        "xt_words": xtp[0],
        "xt_scales": xtp[1],
        "w_words": wp[0],
        "w_scales": wp[1],
        "wb_words": wbp[0],
        "wb_scales": wbp[1],
        "tz": (n((N, E))).astype(np.float32),
        "offs": striped(idx),
        "offs2": striped(idx2),
        "offs3": striped(idx3),
        "offs4": striped(idx4),
        "offs5": striped(idx5),
        "offs6": striped(idx6),
    }


def reference(xt_words, xt_scales, w_words, w_scales, wb_words, wb_scales, tz, offs, offs2, offs3, offs4, offs5, offs6):
    idx = unstriped(offs)
    idx2 = unstriped(offs2)
    idx3 = unstriped(offs3)
    idx4 = unstriped(offs4)
    idx5 = unstriped(offs5)
    idx6 = unstriped(offs6)
    xtu = unpack_weight(xt_words, xt_scales, "e4m3")
    wu = unpack_weight(w_words, w_scales, "e2m1")
    wbu = unpack_weight(wb_words, wb_scales, "e5m2")
    xtidxg = xtu[:, idx]
    a = wu.T @ xtidxg
    xtidx2g = xtu[:, idx2]
    b = wu.T @ xtidx2g
    xtidx3g = xtu[:, idx3]
    g0 = wu.T @ xtidx3g
    c1 = np.maximum(b, g0)
    hid = np.abs(a[:, idx4] - c1[:, idx5])
    hidq = mxq(hid, 0, "e4m3")
    p = wbu.T @ hidq
    y = p + f64(tz)[:, idx6]
    return y

@@ -1,0 +1,165 @@
+from contextlib import ExitStack
+
+import concourse.mybir as mybir
+
+K, T, J, R, O, N, E = 512, 2048, 256, 512, 128, 256, 1024
+FLOPS = 2 * (3 * K * R * J + R * N * O)
+
+F32 = mybir.dt.float32
+BF16 = mybir.dt.bfloat16
+I32 = mybir.dt.int32
+U32 = mybir.dt.uint32
+U16 = mybir.dt.uint16
+U8 = mybir.dt.uint8
+E4M3X4 = mybir.dt.float8_e4m3fn_x4
+E5M2X4 = mybir.dt.float8_e5m2_x4
+E2M1X4 = mybir.dt.float4_e2m1fn_x4
+ALU = mybir.AluOpType
+ACT = mybir.ActivationFunctionType
+
+P = 128
+PACK = 4
+QUADS = 4
+
+
+def load_scale_rows(engines, plane, rows):
+    for q, engine in enumerate(engines):
+        engine.dma_start(out=plane[32 * q : 32 * q + 4, :].bitcast(I32), in_=rows[4 * q : 4 * q + 4, :].bitcast(I32))
+
+
+def tile_list_triple_looked_one_tabled_kernel(
+    tc, xt_words, xt_scales, w_words, w_scales, wb_words, wb_scales, tz, offs, offs2, offs3, offs4, offs5, offs6, out
+):
+    nc = tc.nc
+    with ExitStack() as ctx:
+        lists = ctx.enter_context(tc.tile_pool(name="lists", bufs=1))
+        sb = ctx.enter_context(tc.tile_pool(name="sb", bufs=1))
+        ps = ctx.enter_context(tc.psum_pool(name="ps", bufs=1))
+
+        token_lists = [lists.tile([P, J // 16], U16, name=f"token_list{i}") for i in range(3)]
+        a_list = lists.tile([P, O // 16], U16, name="a_list")
+        c_list = lists.tile([P, O // 16], U16, name="c_list")
+        tz_list = lists.tile([P, O // 16], U16, name="tz_list")
+
+        xt_codes = sb.tile([P, T], U32, name="xt_codes", align_bytes=64)
+        xt_plane = sb.tile([P, T], U8, name="xt_plane", align_bytes=64)
+        w_raw = sb.tile([P, 2 * R], U8, name="w_raw", align_bytes=64)
+        w_raw_plane = sb.tile([P, R], U8, name="w_raw_plane", align_bytes=64)
+        w_codes = sb.tile([P, 2 * R], U8, name="w_codes", align_bytes=64)
+        w_plane = sb.tile([P, R], U8, name="w_plane", align_bytes=64)
+        wb_codes = sb.tile([P, N], U32, name="wb_codes", align_bytes=64)
+        wb_plane = sb.tile([P, N], U8, name="wb_plane", align_bytes=64)
+        tz_table = sb.tile([P, N // P, E], F32, name="tz_table", align_bytes=64)
+
+        for plane in (xt_plane, w_raw_plane, wb_plane):
+            nc.vector.memset(plane[:].bitcast(I32), 0)
+
+        nc.sync.dma_start(token_lists[0][:], offs)
+        nc.sync.dma_start(token_lists[1][:], offs2)
+        nc.sync.dma_start(out=w_raw[:].bitcast(I32), in_=w_words[0].bitcast(I32))
+        load_scale_rows((nc.sync, nc.sync, nc.scalar, nc.scalar), xt_plane, xt_scales[0])
+        nc.sync.dma_start(out=xt_codes[:].bitcast(I32), in_=xt_words[0].rearrange("p n t -> p (n t)").bitcast(I32))
+        load_scale_rows((nc.sync,) * QUADS, w_raw_plane, w_scales[0])
+        nc.sync.dma_start(token_lists[2][:], offs3)
+        nc.sync.dma_start(a_list[:], offs4)
+        nc.sync.dma_start(c_list[:], offs5)
+        nc.sync.dma_start(tz_list[:], offs6)
+        nc.sync.dma_start(out=wb_codes[:].bitcast(I32), in_=wb_words[0].rearrange("p n t -> p (n t)").bitcast(I32))
+        load_scale_rows((nc.sync,) * QUADS, wb_plane, wb_scales[0])
+        nc.sync.dma_start(out=tz_table[:], in_=tz.rearrange("(h p) e -> p h e", p=P))
+
+        got_codes = [sb.tile([P, J], U32, name=f"got_codes{i}", align_bytes=64) for i in range(3)]
+        got_plane = [sb.tile([P, J], U8, name=f"got_plane{i}", align_bytes=64) for i in range(3)]
+
+        def gather_scales(i):
+            nc.vector.tensor_copy(got_plane[i][:], xt_plane[:].indirect(token_lists[i][:]))
+
+        def gather_words(i):
+            nc.vector.tensor_copy(got_codes[i][:], xt_codes[:].indirect(token_lists[i][:]))
+
+        nc.vector.tensor_copy(
+            w_codes[:].bitcast(U16).rearrange("p (t m) -> p t m", t=PACK),
+            w_raw[:].bitcast(U16).rearrange("p (m t) -> p t m", t=PACK),
+        )
+        gather_scales(0)
+        gather_scales(1)
+        gather_words(0)
+        nc.vector.tensor_copy(
+            w_plane[:].rearrange("p (t m) -> p t m", t=PACK),
+            w_raw_plane[:].rearrange("p (m t) -> p t m", t=PACK),
+        )
+        gather_words(1)
+        gather_scales(2)
+        gather_words(2)
+
+        def first_product(dst, i, t):
+            nc.tensor.matmul_mx(
+                out=dst,
+                lhsT=w_codes[:, 2 * P * t : 2 * P * (t + 1)].bitcast(E2M1X4),
+                lhsT_scale=w_plane[:, P * t : P * (t + 1)],
+                rhs=got_codes[i][:].bitcast(E4M3X4),
+                rhs_scale=got_plane[i][:],
+                start=True,
+                stop=True,
+            )
+
+        a_banks = [ps.tile([P, 2, J], F32, name=f"a_bank{u}", tag=f"early{u}") for u in range(2)]
+        b_banks = [ps.tile([P, 2, J], F32, name=f"b_bank{u}") for u in range(2)]
+        g_banks = [ps.tile([P, J], F32, name=f"g_bank{t}") for t in range(PACK)]
+        a_sb = [sb.tile([P, 2, J], F32, name=f"a_sb{u}") for u in range(2)]
+        b_sb = [sb.tile([P, 2, J], F32, name=f"b_sb{u}") for u in range(2)]
+        c_sb = [sb.tile([P, J], F32, name=f"c_sb{t}") for t in range(PACK)]
+        a_got = sb.tile([P, PACK, O], F32, name="a_got")
+        c_got = sb.tile([P, PACK, O], F32, name="c_got", tag="late_got")
+        diff = sb.tile([P, PACK, O], F32, name="diff")
+        hid = sb.tile([P, O, PACK], BF16, name="hid", align_bytes=64)
+        hid_codes = sb.tile([P, O], U32, name="hid_codes", align_bytes=64)
+        hid_plane = sb.tile([P, O], U8, name="hid_plane", align_bytes=64)
+
+        for t in range(PACK):
+            first_product(a_banks[t // 2][:, t % 2, :], 0, t)
+        for u in range(2):
+            nc.scalar.copy(a_sb[u][:], a_banks[u][:])
+        for t in range(PACK):
+            first_product(b_banks[t // 2][:, t % 2, :], 1, t)
+        for u in range(2):
+            nc.scalar.copy(b_sb[u][:], b_banks[u][:])
+        for t in range(PACK):
+            first_product(g_banks[t][:], 2, t)
+        for t in range(PACK):
+            nc.vector.tensor_copy(a_got[:, t, :], a_sb[t // 2][:, t % 2, :].indirect(a_list[:]))
+        for t in range(PACK):
+            nc.vector.tensor_tensor(c_sb[t][:], g_banks[t][:], b_sb[t // 2][:, t % 2, :], ALU.max)
+            nc.scalar.activation(c_got[:, t, :], c_sb[t][:].indirect(c_list[:]), ACT.Copy)
+        for u in range(2):
+            pair = slice(2 * u, 2 * u + 2)
+            nc.vector.tensor_tensor(diff[:, pair, :], a_got[:, pair, :], c_got[:, pair, :], ALU.subtract)
+
+        by_place = diff[:].rearrange("p t o -> p o t")
+        half = O // 2
+        nc.scalar.activation(hid[:, :half, :], by_place[:, :half, :], ACT.Abs)
+        nc.vector.scalar_tensor_tensor(
+            hid[:, half:, :], by_place[:, half:, :], -1.0, by_place[:, half:, :], ALU.mult, ALU.max
+        )
+        nc.vector.quantize_mx(
+            out=hid_codes[:].bitcast(E4M3X4), scales=hid_plane[:], in_=hid[:].rearrange("p o t -> p (o t)")
+        )
+        tz_got = sb.tile([P, N // P, O], F32, name="tz_got", tag="late_got")
+        for h in range(N // P):
+            nc.scalar.activation(tz_got[:, h, :], tz_table[:, h, :].indirect(tz_list[:]), ACT.Copy)
+
+        for h in range(N // P):
+            cols = slice(P * h, P * (h + 1))
+            p_bank = ps.tile([P, O], F32, name=f"p_bank{h}", tag=f"early{h}")
+            nc.tensor.matmul_mx(
+                out=p_bank[:],
+                lhsT=wb_codes[:, cols].bitcast(E5M2X4),
+                lhsT_scale=wb_plane[:, cols],
+                rhs=hid_codes[:].bitcast(E4M3X4),
+                rhs_scale=hid_plane[:],
+                start=True,
+                stop=True,
+            )
+            result = sb.tile([P, O], F32, name=f"result{h}")
+            nc.vector.tensor_tensor(result[:], p_bank[:], tz_got[:, h, :], ALU.add)
+            (nc.sync, nc.scalar)[h].dma_start(out=out[cols, :], in_=result[:])

@@ -44,7 +44,7 @@ def tile_list_triple_looked_one_tabled_kernel(
         xt_codes = sb.tile([P, T], U32, name="xt_codes", align_bytes=64)
         xt_plane = sb.tile([P, T], U8, name="xt_plane", align_bytes=64)
         w_raw = sb.tile([P, 2 * R], U8, name="w_raw", align_bytes=64)
-        w_raw_plane = sb.tile([P, R], U8, name="w_raw_plane", align_bytes=64)
+        w_raw_plane = sb.tile([P, R], U8, name="w_raw_plane", tag="got_b", align_bytes=64)
         w_codes = sb.tile([P, 2 * R], U8, name="w_codes", align_bytes=64)
         w_plane = sb.tile([P, R], U8, name="w_plane", align_bytes=64)
         wb_codes = sb.tile([P, N], U32, name="wb_codes", align_bytes=64)
@@ -54,13 +54,12 @@ def tile_list_triple_looked_one_tabled_kernel(
         for plane in (xt_plane, w_raw_plane, wb_plane):
             nc.vector.memset(plane[:].bitcast(I32), 0)
 
-        nc.sync.dma_start(token_lists[0][:], offs)
-        nc.sync.dma_start(token_lists[1][:], offs2)
-        nc.sync.dma_start(out=w_raw[:].bitcast(I32), in_=w_words[0].bitcast(I32))
+        for tile, src in zip(token_lists, (offs, offs2, offs3)):
+            nc.sync.dma_start(tile[:], src)
         load_scale_rows((nc.sync, nc.sync, nc.scalar, nc.scalar), xt_plane, xt_scales[0])
         nc.sync.dma_start(out=xt_codes[:].bitcast(I32), in_=xt_words[0].rearrange("p n t -> p (n t)").bitcast(I32))
+        nc.sync.dma_start(out=w_raw[:].bitcast(I32), in_=w_words[0].bitcast(I32))
         load_scale_rows((nc.sync,) * QUADS, w_raw_plane, w_scales[0])
-        nc.sync.dma_start(token_lists[2][:], offs3)
         nc.sync.dma_start(a_list[:], offs4)
         nc.sync.dma_start(c_list[:], offs5)
         nc.sync.dma_start(tz_list[:], offs6)
@@ -68,45 +67,38 @@ def tile_list_triple_looked_one_tabled_kernel(
         load_scale_rows((nc.sync,) * QUADS, wb_plane, wb_scales[0])
         nc.sync.dma_start(out=tz_table[:], in_=tz.rearrange("(h p) e -> p h e", p=P))
 
-        got_codes = [sb.tile([P, J], U32, name=f"got_codes{i}", align_bytes=64) for i in range(3)]
         got_plane = [sb.tile([P, J], U8, name=f"got_plane{i}", align_bytes=64) for i in range(3)]
-
-        def gather_scales(i):
+        for i in range(3):
             nc.vector.tensor_copy(got_plane[i][:], xt_plane[:].indirect(token_lists[i][:]))
 
-        def gather_words(i):
-            nc.vector.tensor_copy(got_codes[i][:], xt_codes[:].indirect(token_lists[i][:]))
-
-        nc.vector.tensor_copy(
-            w_codes[:].bitcast(U16).rearrange("p (t m) -> p t m", t=PACK),
-            w_raw[:].bitcast(U16).rearrange("p (m t) -> p t m", t=PACK),
-        )
-        gather_scales(0)
-        gather_scales(1)
-        gather_words(0)
-        nc.vector.tensor_copy(
-            w_plane[:].rearrange("p (t m) -> p t m", t=PACK),
-            w_raw_plane[:].rearrange("p (m t) -> p t m", t=PACK),
-        )
-        gather_words(1)
-        gather_scales(2)
-        gather_words(2)
+        got_a = sb.tile([P, J], U32, name="got_a", align_bytes=64)
+        for u in range(2):
+            nc.scalar.copy(
+                w_codes[:].bitcast(U16).rearrange("p (t m) -> p t m", t=PACK)[:, 2 * u : 2 * u + 2, :],
+                w_raw[:].bitcast(U16).rearrange("p (m t) -> p t m", t=PACK)[:, 2 * u : 2 * u + 2, :],
+            )
+        nc.vector.tensor_copy(got_a[:], xt_codes[:].indirect(token_lists[0][:]))
+        for t in range(PACK):
+            nc.vector.tensor_copy(w_plane[:, P * t : P * (t + 1)], w_raw_plane[:, t::PACK])
+        got_bg = sb.tile([P, 2, J], U32, name="got_bg", tag="got_b", align_bytes=64)
+        for i in range(2):
+            nc.vector.tensor_copy(got_bg[:, i, :], xt_codes[:].indirect(token_lists[1 + i][:]))
+        got_codes = [got_a[:], got_bg[:, 0, :], got_bg[:, 1, :]]
 
         def first_product(dst, i, t):
             nc.tensor.matmul_mx(
                 out=dst,
                 lhsT=w_codes[:, 2 * P * t : 2 * P * (t + 1)].bitcast(E2M1X4),
                 lhsT_scale=w_plane[:, P * t : P * (t + 1)],
-                rhs=got_codes[i][:].bitcast(E4M3X4),
+                rhs=got_codes[i].bitcast(E4M3X4),
                 rhs_scale=got_plane[i][:],
                 start=True,
                 stop=True,
             )
 
-        a_banks = [ps.tile([P, 2, J], F32, name=f"a_bank{u}", tag=f"early{u}") for u in range(2)]
+        a_banks = [ps.tile([P, J], F32, name=f"a_bank{t}", tag=f"bank{t}") for t in range(PACK)]
         b_banks = [ps.tile([P, 2, J], F32, name=f"b_bank{u}") for u in range(2)]
-        g_banks = [ps.tile([P, J], F32, name=f"g_bank{t}") for t in range(PACK)]
-        a_sb = [sb.tile([P, 2, J], F32, name=f"a_sb{u}") for u in range(2)]
+        a_sb = [sb.tile([P, J], F32, name=f"a_sb{t}") for t in range(PACK)]
         b_sb = [sb.tile([P, 2, J], F32, name=f"b_sb{u}") for u in range(2)]
         c_sb = [sb.tile([P, J], F32, name=f"c_sb{t}") for t in range(PACK)]
         a_got = sb.tile([P, PACK, O], F32, name="a_got")
@@ -117,29 +109,28 @@ def tile_list_triple_looked_one_tabled_kernel(
         hid_plane = sb.tile([P, O], U8, name="hid_plane", align_bytes=64)
 
         for t in range(PACK):
-            first_product(a_banks[t // 2][:, t % 2, :], 0, t)
-        for u in range(2):
-            nc.scalar.copy(a_sb[u][:], a_banks[u][:])
+            first_product(a_banks[t][:], 0, t)
+            nc.scalar.copy(a_sb[t][:], a_banks[t][:])
         for t in range(PACK):
             first_product(b_banks[t // 2][:, t % 2, :], 1, t)
         for u in range(2):
             nc.scalar.copy(b_sb[u][:], b_banks[u][:])
         for t in range(PACK):
-            first_product(g_banks[t][:], 2, t)
-        for t in range(PACK):
-            nc.vector.tensor_copy(a_got[:, t, :], a_sb[t // 2][:, t % 2, :].indirect(a_list[:]))
-        for t in range(PACK):
-            nc.vector.tensor_tensor(c_sb[t][:], g_banks[t][:], b_sb[t // 2][:, t % 2, :], ALU.max)
+            nc.vector.tensor_copy(a_got[:, t, :], a_sb[t][:].indirect(a_list[:]))
+        for t, tag in enumerate(("bank4", "bank5", "bank0", "bank1")):
+            g_bank = ps.tile([P, J], F32, name=f"g_bank{t}", tag=tag)
+            first_product(g_bank[:], 2, t)
+            nc.vector.tensor_tensor(c_sb[t][:], g_bank[:], b_sb[t // 2][:, t % 2, :], ALU.max)
             nc.scalar.activation(c_got[:, t, :], c_sb[t][:].indirect(c_list[:]), ACT.Copy)
         for u in range(2):
             pair = slice(2 * u, 2 * u + 2)
             nc.vector.tensor_tensor(diff[:, pair, :], a_got[:, pair, :], c_got[:, pair, :], ALU.subtract)
 
         by_place = diff[:].rearrange("p t o -> p o t")
-        half = O // 2
-        nc.scalar.activation(hid[:, :half, :], by_place[:, :half, :], ACT.Abs)
+        cut = 80
+        nc.scalar.activation(hid[:, :cut, :], by_place[:, :cut, :], ACT.Abs)
         nc.vector.scalar_tensor_tensor(
-            hid[:, half:, :], by_place[:, half:, :], -1.0, by_place[:, half:, :], ALU.mult, ALU.max
+            hid[:, cut:, :], by_place[:, cut:, :], -1.0, by_place[:, cut:, :], ALU.mult, ALU.max
         )
         nc.vector.quantize_mx(
             out=hid_codes[:].bitcast(E4M3X4), scales=hid_plane[:], in_=hid[:].rearrange("p o t -> p (o t)")
@@ -150,7 +141,7 @@ def tile_list_triple_looked_one_tabled_kernel(
 
         for h in range(N // P):
             cols = slice(P * h, P * (h + 1))
-            p_bank = ps.tile([P, O], F32, name=f"p_bank{h}", tag=f"early{h}")
+            p_bank = ps.tile([P, O], F32, name=f"p_bank{h}", tag=f"bank{2 + h}")
             nc.tensor.matmul_mx(
                 out=p_bank[:],
                 lhsT=wb_codes[:, cols].bitcast(E5M2X4),

from contextlib import ExitStack

import concourse.mybir as mybir

K, T, J, R, O, N, E = 512, 2048, 256, 512, 128, 256, 1024
FLOPS = 2 * (3 * K * R * J + R * N * O)

F32 = mybir.dt.float32
BF16 = mybir.dt.bfloat16
I32 = mybir.dt.int32
U32 = mybir.dt.uint32
U16 = mybir.dt.uint16
U8 = mybir.dt.uint8
E4M3X4 = mybir.dt.float8_e4m3fn_x4
E5M2X4 = mybir.dt.float8_e5m2_x4
E2M1X4 = mybir.dt.float4_e2m1fn_x4
ALU = mybir.AluOpType
ACT = mybir.ActivationFunctionType

P = 128
PACK = 4
QUADS = 4


def load_scale_rows(engines, plane, rows):
    for q, engine in enumerate(engines):
        engine.dma_start(out=plane[32 * q : 32 * q + 4, :].bitcast(I32), in_=rows[4 * q : 4 * q + 4, :].bitcast(I32))


def tile_list_triple_looked_one_tabled_kernel(
    tc, xt_words, xt_scales, w_words, w_scales, wb_words, wb_scales, tz, offs, offs2, offs3, offs4, offs5, offs6, out
):
    nc = tc.nc
    with ExitStack() as ctx:
        lists = ctx.enter_context(tc.tile_pool(name="lists", bufs=1))
        sb = ctx.enter_context(tc.tile_pool(name="sb", bufs=1))
        ps = ctx.enter_context(tc.psum_pool(name="ps", bufs=1))

        token_lists = [lists.tile([P, J // 16], U16, name=f"token_list{i}") for i in range(3)]
        a_list = lists.tile([P, O // 16], U16, name="a_list")
        c_list = lists.tile([P, O // 16], U16, name="c_list")
        tz_list = lists.tile([P, O // 16], U16, name="tz_list")

        xt_codes = sb.tile([P, T], U32, name="xt_codes", align_bytes=64)
        xt_plane = sb.tile([P, T], U8, name="xt_plane", align_bytes=64)
        w_raw = sb.tile([P, 2 * R], U8, name="w_raw", align_bytes=64)
        w_raw_plane = sb.tile([P, R], U8, name="w_raw_plane", tag="got_b", align_bytes=64)
        w_codes = sb.tile([P, 2 * R], U8, name="w_codes", align_bytes=64)
        w_plane = sb.tile([P, R], U8, name="w_plane", align_bytes=64)
        wb_codes = sb.tile([P, N], U32, name="wb_codes", align_bytes=64)
        wb_plane = sb.tile([P, N], U8, name="wb_plane", align_bytes=64)
        tz_table = sb.tile([P, N // P, E], F32, name="tz_table", align_bytes=64)

        for plane in (xt_plane, w_raw_plane, wb_plane):
            nc.vector.memset(plane[:].bitcast(I32), 0)

        for tile, src in zip(token_lists, (offs, offs2, offs3)):
            nc.sync.dma_start(tile[:], src)
        load_scale_rows((nc.sync, nc.sync, nc.scalar, nc.scalar), xt_plane, xt_scales[0])
        nc.sync.dma_start(out=xt_codes[:].bitcast(I32), in_=xt_words[0].rearrange("p n t -> p (n t)").bitcast(I32))
        nc.sync.dma_start(out=w_raw[:].bitcast(I32), in_=w_words[0].bitcast(I32))
        load_scale_rows((nc.sync,) * QUADS, w_raw_plane, w_scales[0])
        nc.sync.dma_start(a_list[:], offs4)
        nc.sync.dma_start(c_list[:], offs5)
        nc.sync.dma_start(tz_list[:], offs6)
        nc.sync.dma_start(out=wb_codes[:].bitcast(I32), in_=wb_words[0].rearrange("p n t -> p (n t)").bitcast(I32))
        load_scale_rows((nc.sync,) * QUADS, wb_plane, wb_scales[0])
        nc.sync.dma_start(out=tz_table[:], in_=tz.rearrange("(h p) e -> p h e", p=P))

        got_plane = [sb.tile([P, J], U8, name=f"got_plane{i}", align_bytes=64) for i in range(3)]
        for i in range(3):
            nc.vector.tensor_copy(got_plane[i][:], xt_plane[:].indirect(token_lists[i][:]))

        got_a = sb.tile([P, J], U32, name="got_a", align_bytes=64)
        for u in range(2):
            nc.scalar.copy(
                w_codes[:].bitcast(U16).rearrange("p (t m) -> p t m", t=PACK)[:, 2 * u : 2 * u + 2, :],
                w_raw[:].bitcast(U16).rearrange("p (m t) -> p t m", t=PACK)[:, 2 * u : 2 * u + 2, :],
            )
        nc.vector.tensor_copy(got_a[:], xt_codes[:].indirect(token_lists[0][:]))
        for t in range(PACK):
            nc.vector.tensor_copy(w_plane[:, P * t : P * (t + 1)], w_raw_plane[:, t::PACK])
        got_bg = sb.tile([P, 2, J], U32, name="got_bg", tag="got_b", align_bytes=64)
        for i in range(2):
            nc.vector.tensor_copy(got_bg[:, i, :], xt_codes[:].indirect(token_lists[1 + i][:]))
        got_codes = [got_a[:], got_bg[:, 0, :], got_bg[:, 1, :]]

        def first_product(dst, i, t):
            nc.tensor.matmul_mx(
                out=dst,
                lhsT=w_codes[:, 2 * P * t : 2 * P * (t + 1)].bitcast(E2M1X4),
                lhsT_scale=w_plane[:, P * t : P * (t + 1)],
                rhs=got_codes[i].bitcast(E4M3X4),
                rhs_scale=got_plane[i][:],
                start=True,
                stop=True,
            )

        a_banks = [ps.tile([P, J], F32, name=f"a_bank{t}", tag=f"bank{t}") for t in range(PACK)]
        b_banks = [ps.tile([P, 2, J], F32, name=f"b_bank{u}") for u in range(2)]
        a_sb = [sb.tile([P, J], F32, name=f"a_sb{t}") for t in range(PACK)]
        b_sb = [sb.tile([P, 2, J], F32, name=f"b_sb{u}") for u in range(2)]
        c_sb = [sb.tile([P, J], F32, name=f"c_sb{t}") for t in range(PACK)]
        a_got = sb.tile([P, PACK, O], F32, name="a_got")
        c_got = sb.tile([P, PACK, O], F32, name="c_got", tag="late_got")
        diff = sb.tile([P, PACK, O], F32, name="diff")
        hid = sb.tile([P, O, PACK], BF16, name="hid", align_bytes=64)
        hid_codes = sb.tile([P, O], U32, name="hid_codes", align_bytes=64)
        hid_plane = sb.tile([P, O], U8, name="hid_plane", align_bytes=64)

        for t in range(PACK):
            first_product(a_banks[t][:], 0, t)
            nc.scalar.copy(a_sb[t][:], a_banks[t][:])
        for t in range(PACK):
            first_product(b_banks[t // 2][:, t % 2, :], 1, t)
        for u in range(2):
            nc.scalar.copy(b_sb[u][:], b_banks[u][:])
        for t in range(PACK):
            nc.vector.tensor_copy(a_got[:, t, :], a_sb[t][:].indirect(a_list[:]))
        for t, tag in enumerate(("bank4", "bank5", "bank0", "bank1")):
            g_bank = ps.tile([P, J], F32, name=f"g_bank{t}", tag=tag)
            first_product(g_bank[:], 2, t)
            nc.vector.tensor_tensor(c_sb[t][:], g_bank[:], b_sb[t // 2][:, t % 2, :], ALU.max)
            nc.scalar.activation(c_got[:, t, :], c_sb[t][:].indirect(c_list[:]), ACT.Copy)
        for u in range(2):
            pair = slice(2 * u, 2 * u + 2)
            nc.vector.tensor_tensor(diff[:, pair, :], a_got[:, pair, :], c_got[:, pair, :], ALU.subtract)

        by_place = diff[:].rearrange("p t o -> p o t")
        cut = 80
        nc.scalar.activation(hid[:, :cut, :], by_place[:, :cut, :], ACT.Abs)
        nc.vector.scalar_tensor_tensor(
            hid[:, cut:, :], by_place[:, cut:, :], -1.0, by_place[:, cut:, :], ALU.mult, ALU.max
        )
        nc.vector.quantize_mx(
            out=hid_codes[:].bitcast(E4M3X4), scales=hid_plane[:], in_=hid[:].rearrange("p o t -> p (o t)")
        )
        tz_got = sb.tile([P, N // P, O], F32, name="tz_got", tag="late_got")
        for h in range(N // P):
            nc.scalar.activation(tz_got[:, h, :], tz_table[:, h, :].indirect(tz_list[:]), ACT.Copy)

        for h in range(N // P):
            cols = slice(P * h, P * (h + 1))
            p_bank = ps.tile([P, O], F32, name=f"p_bank{h}", tag=f"bank{2 + h}")
            nc.tensor.matmul_mx(
                out=p_bank[:],
                lhsT=wb_codes[:, cols].bitcast(E5M2X4),
                lhsT_scale=wb_plane[:, cols],
                rhs=hid_codes[:].bitcast(E4M3X4),
                rhs_scale=hid_plane[:],
                start=True,
                stop=True,
            )
            result = sb.tile([P, O], F32, name=f"result{h}")
            nc.vector.tensor_tensor(result[:], p_bank[:], tz_got[:, h, :], ALU.add)
            (nc.sync, nc.scalar)[h].dma_start(out=out[cols, :], in_=result[:])
